import numpy as np
import ml_dtypes


def mxq(x, axis, fmt="e4m3"):
    dtype, down = {"e4m3": (ml_dtypes.float8_e4m3fn, 7), "e5m2": (ml_dtypes.float8_e5m2, 14)}[fmt]
    v = np.moveaxis(np.asarray(x, np.float32).astype(ml_dtypes.bfloat16).astype(np.float64), axis, -1)
    blocks = v.reshape(v.shape[:-1] + (-1, 32))
    amax = np.abs(blocks).max(-1, keepdims=True)
    byte = np.maximum(np.where(amax > 0, np.frexp(amax)[1] - 1 + 127, 0) - down, 1)
    scale = np.exp2(byte - 127.0)
    codes = (blocks / scale).astype(np.float32).astype(dtype).astype(np.float64)
    return np.moveaxis((codes * scale).reshape(v.shape), -1, axis)


WIDE = False


def mx_kscale(k):
    if not WIDE:
        return np.ones(k)
    levels = np.array([10, -10, 5, -5, 0])
    if k % 512:
        return np.exp2(np.random.permutation(np.resize(levels, k // 32))).repeat(32)
    a = np.empty((k // 512, 16))
    for p in range(k // 512):
        a[p, :8] = np.random.permutation(np.resize(levels, 8))
        for g in range(8):
            far = levels[np.abs(levels - a[p, g]) >= 10]
            a[p, g + 8] = far[np.random.randint(len(far))]
    return np.exp2(a.ravel()).repeat(32)


def f64(x):
    return np.asarray(x).astype(np.float64)


def striped(idx):
    return np.tile(idx.reshape(-1, 16).T, (8, 1)).astype(np.uint16)


def unstriped(offs):
    return offs[:16].T.reshape(-1).astype(np.int64)


E2M1 = np.array([0.0, 0.5, 1.0, 1.5, 2.0, 3.0, 4.0, 6.0, -0.0, -0.5, -1.0, -1.5, -2.0, -3.0, -4.0, -6.0])


def pack_weight(w, fmt):
    k, n = w.shape
    w = f64(np.asarray(w, np.float32).astype(ml_dtypes.bfloat16)).reshape(k // 32, 32, n)
    amax = np.abs(w).max(1)
    if fmt == "e4m3":
        byte = np.frexp(amax)[1] - 1 + 127 - 7
    else:
        mant, ex = np.frexp(amax / 6.0)
        byte = np.where(mant > 0.5, ex, ex - 1) + 127
    byte = np.clip(np.where(amax > 0, byte, 1), 1, 254)
    scaled = (w * np.exp2(127.0 - byte)[:, None, :]).reshape(k, n).astype(np.float32)
    by_word = np.ascontiguousarray(scaled.reshape(k // 512, 128, 4, n).transpose(0, 1, 3, 2))
    if fmt == "e4m3":
        words = by_word.astype(ml_dtypes.float8_e4m3fn).view(np.uint8)
    else:
        c = by_word.astype(ml_dtypes.float4_e2m1fn).view(np.uint8) & 0xF
        words = (c[..., 0::2] | (c[..., 1::2] << 4)).reshape(k // 512, 128, 2 * n)
    return np.ascontiguousarray(words), np.ascontiguousarray(byte.astype(np.uint8).reshape(k // 512, 16, n))


def unpack_weight(words, scales, fmt):
    g, _, n = scales.shape
    words = np.ascontiguousarray(words).reshape(g, 128, n, -1)
    if fmt == "e4m3":
        vals = words.view(ml_dtypes.float8_e4m3fn).astype(np.float64)
    else:
        nib = np.empty((g, 128, n, 4), np.uint8)
        nib[..., 0::2] = words & 0xF
        nib[..., 1::2] = words >> 4
        vals = E2M1[nib]
    vals = vals * np.repeat(np.exp2(scales.astype(np.float64) - 127.0), 8, axis=1)[..., None]
    return vals.transpose(0, 1, 3, 2).reshape(g * 512, n)


def gelu(v):
    return 0.5 * v * (1.0 + np.tanh(np.sqrt(2.0 / np.pi) * (v + 0.044715 * v**3)))


def twice(P):
    return np.random.permutation(np.repeat(np.arange(P), 2))


K, H, H2, T, S, P = 1536, 512, 1024, 4096, 1024, 512

def setup_inputs():
    n = np.random.standard_normal
    s = mx_kscale(K)[:, None]
    u = mx_kscale(H)[:, None]
    d = {}
    d["tab_words"], d["tab_scales"] = pack_weight(n((K, T)) * s, "e4m3")
    d["offs"] = striped(np.random.permutation(T)[:S])
    d["w1"] = (n((K, H2)) / s * np.tile(u, (H2 // H, 1)).T / K ** 0.5).astype(np.float32)
    d["pos1"] = striped(np.random.permutation(S)[:P])
    d["pos2"] = striped(np.random.permutation(S)[:P])
    d["w2_words"], d["w2_scales"] = pack_weight(1.5 * n((H, H)) / u / H ** 0.5, "e2m1")
    d["pos3"] = striped(twice(P))
    sign = np.random.choice([-1.0, 1.0], H)
    d["tune"] = (sign * np.random.uniform(0.45, 0.55, H) / u[:, 0]).astype(np.float32)
    return d

def reference(tab_words, tab_scales, offs, w1, pos1, pos2, w2_words, w2_scales, pos3, tune):
    v = unpack_weight(tab_words, tab_scales, "e4m3")[:, unstriped(offs)]
    mag = np.abs(mxq(f64(w1), 0, "e4m3").T @ v)
    h = mag[:H] - mag[H:]
    x = np.maximum(h[:, unstriped(pos1)], h[:, unstriped(pos2)])
    w2 = unpack_weight(w2_words, w2_scales, "e2m1")
    y = w2.T @ mxq(x, 0, "e4m3")
    up = np.tanh(y[:, unstriped(pos3)])
    return up * np.sin(f64(tune)[:, None] * h)

@@ -1,0 +1,234 @@
+import math
+from contextlib import ExitStack
+
+import concourse.mybir as mybir
+
+K, H, T, S, PAIRS = 1536, 512, 4096, 1024, 512
+P = 128
+PACK = 4
+K_PASS = P * PACK
+PASSES = K // K_PASS
+TILES = H // P
+BANK = 512
+
+FLOPS = 2 * K * (2 * H) * S + 2 * H * H * PAIRS
+
+F32 = mybir.dt.float32
+BF16 = mybir.dt.bfloat16
+I32 = mybir.dt.int32
+U32 = mybir.dt.uint32
+U16 = mybir.dt.uint16
+U8 = mybir.dt.uint8
+FP8X4 = mybir.dt.float8_e4m3fn_x4
+FP4X4 = mybir.dt.float4_e2m1fn_x4
+ALU = mybir.AluOpType
+ACT = mybir.ActivationFunctionType
+
+
+def tile_list_blade_noise_scores_kernel(
+    tc, tab_words, tab_scales, offs, w1, pos1, pos2, w2_words, w2_scales, pos3, tune, out
+):
+    nc = tc.nc
+    with ExitStack() as ctx:
+        keep = ctx.enter_context(tc.tile_pool(name="keep", bufs=1))
+        work = ctx.enter_context(tc.tile_pool(name="work", bufs=2))
+        psum = ctx.enter_context(tc.psum_pool(name="psum", bufs=8))
+
+        idx = keep.tile([P, S // 16], U16, name="idx")
+        p1 = keep.tile([P, PAIRS // 16], U16, name="p1")
+        p2 = keep.tile([P, PAIRS // 16], U16, name="p2")
+        p3 = keep.tile([P, S // 16], U16, name="p3")
+
+        tab_plane = keep.tile([P, T], U8, name="tab_plane", align_bytes=64)
+        w2_plane = keep.tile([P, H], U8, name="w2_plane", align_bytes=64)
+        nc.vector.memset(tab_plane[:].bitcast(I32), 0)
+        nc.vector.memset(w2_plane[:].bitcast(I32), 0)
+        for quad in range(4):
+            nc.sync.dma_start(
+                out=tab_plane[32 * quad : 32 * quad + 4 * PASSES, :].bitcast(I32),
+                in_=tab_scales[:, 4 * quad : 4 * quad + 4, :].bitcast(I32),
+            )
+
+        table = [keep.tile([P, T], I32, name=f"table{a}", tag=f"table{a}", align_bytes=64) for a in range(PASSES)]
+        w1_raw = [
+            [keep.tile([P, PACK, 2, P], F32, name=f"w1_raw{t}_{a}", tag=f"raw{3 * t + a}", align_bytes=64) for a in range(PASSES)] for t in range(TILES)
+        ]
+
+        def load_table(a):
+            nc.sync.dma_start(out=table[a][:], in_=tab_words[a].rearrange("p t i -> p (t i)").bitcast(I32))
+
+        def load_w1(t):
+            for a in range(PASSES):
+                rows = w1[a * K_PASS : (a + 1) * K_PASS, :].rearrange("(p j) (u c) -> p (j u) c", j=PACK, u=2)
+                nc.sync.dma_start(
+                    out=w1_raw[t][a][:].rearrange("p j u c -> p (j u) c"), in_=rows[:, :, t * P : (t + 1) * P]
+                )
+
+        load_table(0)
+        nc.sync.dma_start(idx[:], offs)
+        load_w1(0)
+        load_table(1)
+        nc.sync.dma_start(p1[:], pos1)
+        nc.sync.dma_start(p2[:], pos2)
+        tune_sb = keep.tile([P, TILES], F32, name="tune_sb")
+        with nc.allow_non_contiguous_dma(reason="512 values, one a partition"):
+            nc.sync.dma_start(out=tune_sb[:], in_=tune.rearrange("(t p) -> p t", p=P))
+        load_table(2)
+        load_w1(1)
+        load_w1(2)
+        load_w1(3)
+        nc.sync.dma_start(p3[:], pos3)
+        w2_codes = keep.tile([P, 2 * H], U8, name="w2_codes", align_bytes=64)
+        nc.sync.dma_start(out=w2_codes[:].bitcast(I32), in_=w2_words[0].bitcast(I32))
+        for quad in range(4):
+            nc.sync.dma_start(
+                out=w2_plane[32 * quad : 32 * quad + 4, :].bitcast(I32),
+                in_=w2_scales[0, 4 * quad : 4 * quad + 4, :].bitcast(I32),
+            )
+
+        v_plane = keep.tile([P, S], U8, name="v_plane", align_bytes=64)
+        v_codes = [keep.tile([P, S], U32, name=f"v_codes{a}", align_bytes=64) for a in range(PASSES)]
+        w1_codes = [
+            [
+                keep.tile([P, 2 * P], U32, name=f"w1_codes{t}_{a}", align_bytes=64, tag=f"codes{3 * t + a}")
+                for a in range(PASSES)
+            ]
+            for t in range(TILES)
+        ]
+        w1_plane = [
+            [keep.tile([P, 2 * P], U8, name=f"w1_plane{t}_{a}", align_bytes=64, tag=f"plane{3 * t + a}") for a in range(PASSES)]
+            for t in range(TILES)
+        ]
+
+        def gather_table(a):
+            for half in range(2):
+                nc.vector.tensor_copy(
+                    v_codes[a][:, half * BANK : (half + 1) * BANK],
+                    table[a][:].bitcast(U32).indirect(idx[:, half * 32 : (half + 1) * 32]),
+                )
+
+        grouped_tag = {3: "table2", 4: "codes2", 5: "plane2"}
+
+        def quantize_w1(n):
+            t, a = divmod(n, PASSES)
+            tag = f"grouped{n}" if n < PASSES else grouped_tag.get(n, f"raw{n - 2}")
+            grouped = keep.tile([P, 2 * P, PACK], BF16, name=f"grouped{n}", align_bytes=64, tag=tag)
+            dst = grouped[:].rearrange("p (c i) j -> p c j i", i=4)
+            src = w1_raw[t][a][:].rearrange("p j u (c i) -> p (u c) j i", i=4)
+            if n <= PASSES:
+                nc.vector.tensor_copy(out=dst, in_=src)
+            else:
+                nc.scalar.copy(out=dst, in_=src)
+            nc.vector.quantize_mx(
+                out=w1_codes[t][a][:].bitcast(FP8X4),
+                scales=w1_plane[t][a][:],
+                in_=grouped[:].rearrange("p c j -> p (c j)"),
+            )
+
+        nc.vector.tensor_copy(v_plane[:], tab_plane[:].indirect(idx[:]))
+        gather_table(0)
+        for n in range(PASSES):
+            quantize_w1(n)
+        gather_table(1)
+        gather_table(2)
+
+        h = [keep.tile([P, S], F32, name=f"h{t}") for t in range(TILES)]
+        x_rows = keep.tile([P, PACK, PAIRS], BF16, name="x_rows", align_bytes=64)
+        turns_per_h = keep.tile([P, TILES], F32, name="turns_per_h")
+        nc.vector.tensor_scalar(turns_per_h[:], tune_sb[:], 1.0 / (2.0 * math.pi), None, ALU.mult)
+        turns = keep.tile([P, TILES * S], F32, name="turns", tag="table1", align_bytes=64)
+
+        def contrast(t):
+            tags = [f"raw{3 * t + 3}" if t in (1, 2) else f"mag{t % 2}_0", f"mag{t % 2}_1"]
+            mag = [keep.tile([P, S], F32, name=f"mag{u}", align_bytes=64, tag=tags[u]) for u in range(2)]
+            for half in range(2):
+                cols = slice(half * BANK, (half + 1) * BANK)
+                for u in range(2):
+                    acc = psum.tile([P, BANK], F32, name="acc")
+                    for a in range(PASSES):
+                        nc.tensor.matmul_mx(
+                            out=acc[:],
+                            lhsT=w1_codes[t][a][:, u * P : (u + 1) * P].bitcast(FP8X4),
+                            lhsT_scale=w1_plane[t][a][:, u * P : (u + 1) * P],
+                            rhs=v_codes[a][:, cols].bitcast(FP8X4),
+                            rhs_scale=v_plane[4 * a :, cols],
+                            start=(a == 0),
+                            stop=(a == PASSES - 1),
+                        )
+                    nc.scalar.activation(out=mag[u][:, cols], in_=acc[:], func=ACT.Abs)
+                nc.vector.tensor_tensor(h[t][:, cols], mag[0][:, cols], mag[1][:, cols], ALU.subtract)
+
+        def pairs(t):
+            pick1 = keep.tile([P, PAIRS], F32, name="pick1", tag="pick0", align_bytes=64)
+            pick2 = keep.tile([P, PAIRS], F32, name="pick2", tag=["plane2", "raw6", "raw9", "pick1"][t], align_bytes=64)
+            nc.vector.tensor_copy(pick1[:], h[t][:].indirect(p1[:]))
+            nc.vector.tensor_copy(pick2[:], h[t][:].indirect(p2[:]))
+            x_tile = keep.tile([P, PAIRS], BF16, name="x_tile", tag=f"x{t}", align_bytes=64)
+            nc.vector.tensor_tensor(x_tile[:], pick1[:], pick2[:], ALU.max)
+            for i in range(PACK):
+                nc.sync.dma_start(out=x_rows[32 * t : 32 * (t + 1), i, :], in_=x_tile[i:P:PACK, :])
+
+        def reduce_turns(t):
+            whole = keep.tile([P, S], I32, name="whole", tag=("pick1" if t == 3 else "pick0"), align_bytes=64)
+            nc.vector.tensor_scalar(whole[:], h[t][:], turns_per_h[:, t : t + 1], None, ALU.mult)
+            nc.vector.scalar_tensor_tensor(
+                turns[:, t * S : (t + 1) * S], h[t][:], turns_per_h[:, t : t + 1], whole[:], ALU.mult, ALU.subtract
+            )
+
+        done = PASSES
+        for t in range(TILES):
+            contrast(t)
+            upto = min(PASSES * (t + 2) + 1, PASSES * TILES)
+            for n in range(done, upto):
+                quantize_w1(n)
+            done = upto
+            pairs(t)
+            if t < 2:
+                reduce_turns(t)
+        reduce_turns(2)
+        reduce_turns(3)
+
+        wave = [keep.tile([P, S], F32, name=f"wave{t}", align_bytes=64, tag=["codes11", "plane11", "wave2", "wave3"][t]) for t in range(TILES)]
+        for t in range(TILES):
+            nc.scalar.activation(out=wave[t][:], in_=turns[:, t * S : (t + 1) * S], func=ACT.Sin, scale=2.0 * math.pi)
+
+        x_grouped = keep.tile([P, PAIRS, PACK], BF16, name="x_grouped", align_bytes=64)
+        nc.vector.tensor_copy(
+            out=x_grouped[:].rearrange("p (c i) j -> p c j i", i=4),
+            in_=x_rows[:].rearrange("p j (c i) -> p c j i", i=4),
+        )
+        x_codes = keep.tile([P, PAIRS], U32, name="x_codes", align_bytes=64)
+        x_plane = keep.tile([P, PAIRS], U8, name="x_plane", align_bytes=64)
+
+        nc.vector.quantize_mx(
+            out=x_codes[:].bitcast(FP8X4), scales=x_plane[:], in_=x_grouped[:].rearrange("p c j -> p (c j)")
+        )
+        y = []
+        for t in range(TILES):
+            acc = psum.tile([P, BANK], F32, name="acc")
+            nc.tensor.matmul_mx(
+                out=acc[:],
+                lhsT=w2_codes[:, 2 * t * P : 2 * (t + 1) * P].bitcast(FP4X4),
+                lhsT_scale=w2_plane[:, t * P : (t + 1) * P],
+                rhs=x_codes[:].bitcast(FP8X4),
+                rhs_scale=x_plane[:],
+                start=True,
+                stop=True,
+            )
+            y_t = keep.tile([P, PAIRS], F32, name=f"y{t}")
+            nc.scalar.copy(out=y_t[:], in_=acc[:])
+            y.append(y_t)
+
+        up_all = keep.tile([P, TILES * S], F32, name="up_all", tag="table0", align_bytes=64)
+        for t in range(TILES):
+            for half in range(2):
+                cols = slice(half * BANK, (half + 1) * BANK)
+                up = up_all[:, t * S + half * BANK : t * S + (half + 1) * BANK]
+                for quarter in range(2):
+                    first = 32 * half + 16 * quarter
+                    nc.vector.tensor_copy(
+                        up[:, quarter * 256 : (quarter + 1) * 256], y[t][:].indirect(p3[:, first : first + 16])
+                    )
+                nc.scalar.activation(out=up, in_=up, func=ACT.Tanh)
+                nc.vector.tensor_tensor(wave[t][:, cols], wave[t][:, cols], up, ALU.mult)
+                nc.sync.dma_start(out=out[t * P : (t + 1) * P, cols], in_=wave[t][:, cols])

@@ -136,10 +136,11 @@ def tile_list_blade_noise_scores_kernel(
         x_rows = keep.tile([P, PACK, PAIRS], BF16, name="x_rows", align_bytes=64)
         turns_per_h = keep.tile([P, TILES], F32, name="turns_per_h")
         nc.vector.tensor_scalar(turns_per_h[:], tune_sb[:], 1.0 / (2.0 * math.pi), None, ALU.mult)
-        turns = keep.tile([P, TILES * S], F32, name="turns", tag="table1", align_bytes=64)
+        whole_all = keep.tile([P, TILES * S], I32, name="whole_all", tag="table1", align_bytes=64)
+        turns = []
 
         def contrast(t):
-            tags = [f"raw{3 * t + 3}" if t in (1, 2) else f"mag{t % 2}_0", f"mag{t % 2}_1"]
+            tags = [f"raw{3 * t + 4}" if t in (1, 2) else f"mag{t % 2}_0", f"mag{t % 2}_1"]
             mag = [keep.tile([P, S], F32, name=f"mag{u}", align_bytes=64, tag=tags[u]) for u in range(2)]
             for half in range(2):
                 cols = slice(half * BANK, (half + 1) * BANK)
@@ -168,29 +169,36 @@ def tile_list_blade_noise_scores_kernel(
             for i in range(PACK):
                 nc.sync.dma_start(out=x_rows[32 * t : 32 * (t + 1), i, :], in_=x_tile[i:P:PACK, :])
 
-        def reduce_turns(t):
-            whole = keep.tile([P, S], I32, name="whole", tag=("pick1" if t == 3 else "pick0"), align_bytes=64)
-            nc.vector.tensor_scalar(whole[:], h[t][:], turns_per_h[:, t : t + 1], None, ALU.mult)
-            nc.vector.scalar_tensor_tensor(
-                turns[:, t * S : (t + 1) * S], h[t][:], turns_per_h[:, t : t + 1], whole[:], ALU.mult, ALU.subtract
+        def whole_turns(t):
+            nc.gpsimd.tensor_scalar(
+                whole_all[:, t * S : (t + 1) * S], h[t][:], turns_per_h[:, t : t + 1], 0.0, ALU.mult, ALU.add
             )
+
+        def reduce_turns(t, dst):
+            nc.vector.scalar_tensor_tensor(
+                dst, h[t][:], turns_per_h[:, t : t + 1], whole_all[:, t * S : (t + 1) * S], ALU.mult, ALU.subtract
+            )
+            turns.append(dst)
 
         done = PASSES
         for t in range(TILES):
             contrast(t)
-            upto = min(PASSES * (t + 2) + 1, PASSES * TILES)
+            whole_turns(t)
+            upto = min(PASSES * (t + 2) + 2, PASSES * TILES)
             for n in range(done, upto):
                 quantize_w1(n)
             done = upto
             pairs(t)
-            if t < 2:
-                reduce_turns(t)
-        reduce_turns(2)
-        reduce_turns(3)
+            if t == 0:
+                turns_first = keep.tile([P, S], F32, name="turns_first", tag="plane2", align_bytes=64)
+                reduce_turns(0, turns_first[:])
+        turns_rest = keep.tile([P, (TILES - 1) * S], F32, name="turns_rest", tag="pick0", align_bytes=64)
+        for t in range(1, TILES):
+            reduce_turns(t, turns_rest[:, (t - 1) * S : t * S])
 
-        wave = [keep.tile([P, S], F32, name=f"wave{t}", align_bytes=64, tag=["codes11", "plane11", "wave2", "wave3"][t]) for t in range(TILES)]
+        wave = [keep.tile([P, S], F32, name=f"wave{t}", align_bytes=64, tag=["codes11", "wave1", "wave2", "wave3"][t]) for t in range(TILES)]
         for t in range(TILES):
-            nc.scalar.activation(out=wave[t][:], in_=turns[:, t * S : (t + 1) * S], func=ACT.Sin, scale=2.0 * math.pi)
+            nc.scalar.activation(out=wave[t][:], in_=turns[t], func=ACT.Sin, scale=2.0 * math.pi)
 
         x_grouped = keep.tile([P, PAIRS, PACK], BF16, name="x_grouped", align_bytes=64)
         nc.vector.tensor_copy(
@@ -203,8 +211,9 @@ def tile_list_blade_noise_scores_kernel(
         nc.vector.quantize_mx(
             out=x_codes[:].bitcast(FP8X4), scales=x_plane[:], in_=x_grouped[:].rearrange("p c j -> p (c j)")
         )
-        y = []
-        for t in range(TILES):
+        y = [keep.tile([P, PAIRS], F32, name=f"y{t}") for t in range(TILES)]
+
+        def second_stage(t):
             acc = psum.tile([P, BANK], F32, name="acc")
             nc.tensor.matmul_mx(
                 out=acc[:],
@@ -215,12 +224,13 @@ def tile_list_blade_noise_scores_kernel(
                 start=True,
                 stop=True,
             )
-            y_t = keep.tile([P, PAIRS], F32, name=f"y{t}")
-            nc.scalar.copy(out=y_t[:], in_=acc[:])
-            y.append(y_t)
+            nc.scalar.copy(out=y[t][:], in_=acc[:])
 
         up_all = keep.tile([P, TILES * S], F32, name="up_all", tag="table0", align_bytes=64)
+        second_stage(0)
         for t in range(TILES):
+            if t + 1 < TILES:
+                second_stage(t + 1)
             for half in range(2):
                 cols = slice(half * BANK, (half + 1) * BANK)
                 up = up_all[:, t * S + half * BANK : t * S + (half + 1) * BANK]
@@ -230,5 +240,6 @@ def tile_list_blade_noise_scores_kernel(
                         up[:, quarter * 256 : (quarter + 1) * 256], y[t][:].indirect(p3[:, first : first + 16])
                     )
                 nc.scalar.activation(out=up, in_=up, func=ACT.Tanh)
-                nc.vector.tensor_tensor(wave[t][:, cols], wave[t][:, cols], up, ALU.mult)
+                engine = nc.gpsimd if t + 1 < TILES else nc.vector
+                engine.tensor_tensor(wave[t][:, cols], wave[t][:, cols], up, ALU.mult)
                 nc.sync.dma_start(out=out[t * P : (t + 1) * P, cols], in_=wave[t][:, cols])

@@ -9,7 +9,13 @@ PACK = 4
 K_PASS = P * PACK
 PASSES = K // K_PASS
 TILES = H // P
+STEPS = TILES * PASSES
+LEAD = 2
 BANK = 512
+QUADS = 4
+PER_COL = 16
+UP_SLICE = PAIRS // 2
+RUN = 4
 
 FLOPS = 2 * K * (2 * H) * S + 2 * H * H * PAIRS
 
@@ -30,127 +36,121 @@ def tile_list_blade_noise_scores_kernel(
 ):
     nc = tc.nc
     with ExitStack() as ctx:
-        keep = ctx.enter_context(tc.tile_pool(name="keep", bufs=1))
-        work = ctx.enter_context(tc.tile_pool(name="work", bufs=2))
+        sbuf = ctx.enter_context(tc.tile_pool(name="sbuf", bufs=1))
         psum = ctx.enter_context(tc.psum_pool(name="psum", bufs=8))
 
-        idx = keep.tile([P, S // 16], U16, name="idx")
-        p1 = keep.tile([P, PAIRS // 16], U16, name="p1")
-        p2 = keep.tile([P, PAIRS // 16], U16, name="p2")
-        p3 = keep.tile([P, S // 16], U16, name="p3")
+        def buffer(tag, shape, dtype):
+            return sbuf.tile(shape, dtype, name=tag, tag=tag, align_bytes=64)
 
-        tab_plane = keep.tile([P, T], U8, name="tab_plane", align_bytes=64)
-        w2_plane = keep.tile([P, H], U8, name="w2_plane", align_bytes=64)
+        idx = sbuf.tile([P, S // PER_COL], U16, name="idx")
+        p1 = sbuf.tile([P, PAIRS // PER_COL], U16, name="p1")
+        p2 = sbuf.tile([P, PAIRS // PER_COL], U16, name="p2")
+        p3 = sbuf.tile([P, S // PER_COL], U16, name="p3")
+
+        tab_plane = buffer("tab_plane", [P, T], U8)
+        w2_plane = buffer("w2_plane", [P, H], U8)
         nc.vector.memset(tab_plane[:].bitcast(I32), 0)
         nc.vector.memset(w2_plane[:].bitcast(I32), 0)
-        for quad in range(4):
+        for quad in range(QUADS):
             nc.sync.dma_start(
                 out=tab_plane[32 * quad : 32 * quad + 4 * PASSES, :].bitcast(I32),
                 in_=tab_scales[:, 4 * quad : 4 * quad + 4, :].bitcast(I32),
             )
 
-        table = [keep.tile([P, T], I32, name=f"table{a}", tag=f"table{a}", align_bytes=64) for a in range(PASSES)]
-        w1_raw = [
-            [keep.tile([P, PACK, 2, P], F32, name=f"w1_raw{t}_{a}", tag=f"raw{3 * t + a}", align_bytes=64) for a in range(PASSES)] for t in range(TILES)
-        ]
+        table = [buffer(f"table{a}", [P, T], I32) for a in range(PASSES)]
+        w1_raw = [buffer(f"raw{n}", [P, PACK, 2, P], F32) for n in range(STEPS)]
 
         def load_table(a):
             nc.sync.dma_start(out=table[a][:], in_=tab_words[a].rearrange("p t i -> p (t i)").bitcast(I32))
 
         def load_w1(t):
             for a in range(PASSES):
-                rows = w1[a * K_PASS : (a + 1) * K_PASS, :].rearrange("(p j) (u c) -> p (j u) c", j=PACK, u=2)
+                rows = w1[a * K_PASS : (a + 1) * K_PASS, :].rearrange("(p i) (u c) -> p (i u) c", i=PACK, u=2)
                 nc.sync.dma_start(
-                    out=w1_raw[t][a][:].rearrange("p j u c -> p (j u) c"), in_=rows[:, :, t * P : (t + 1) * P]
+                    out=w1_raw[PASSES * t + a][:].rearrange("p i u c -> p (i u) c"),
+                    in_=rows[:, :, t * P : (t + 1) * P],
                 )
 
         load_table(0)
         nc.sync.dma_start(idx[:], offs)
         load_w1(0)
-        load_table(1)
+        for a in range(1, PASSES):
+            load_table(a)
         nc.sync.dma_start(p1[:], pos1)
         nc.sync.dma_start(p2[:], pos2)
-        tune_sb = keep.tile([P, TILES], F32, name="tune_sb")
-        with nc.allow_non_contiguous_dma(reason="512 values, one a partition"):
+        tune_sb = sbuf.tile([P, TILES], F32, name="tune_sb")
+        with nc.allow_non_contiguous_dma(reason="512 values: tune[128 t + p] goes to [p, t]"):
             nc.sync.dma_start(out=tune_sb[:], in_=tune.rearrange("(t p) -> p t", p=P))
-        load_table(2)
-        load_w1(1)
-        load_w1(2)
-        load_w1(3)
+        for t in range(1, TILES):
+            load_w1(t)
         nc.sync.dma_start(p3[:], pos3)
-        w2_codes = keep.tile([P, 2 * H], U8, name="w2_codes", align_bytes=64)
+        w2_codes = buffer("w2_codes", [P, 2 * H], U8)
         nc.sync.dma_start(out=w2_codes[:].bitcast(I32), in_=w2_words[0].bitcast(I32))
-        for quad in range(4):
+        for quad in range(QUADS):
             nc.sync.dma_start(
                 out=w2_plane[32 * quad : 32 * quad + 4, :].bitcast(I32),
                 in_=w2_scales[0, 4 * quad : 4 * quad + 4, :].bitcast(I32),
             )
 
-        v_plane = keep.tile([P, S], U8, name="v_plane", align_bytes=64)
-        v_codes = [keep.tile([P, S], U32, name=f"v_codes{a}", align_bytes=64) for a in range(PASSES)]
-        w1_codes = [
-            [
-                keep.tile([P, 2 * P], U32, name=f"w1_codes{t}_{a}", align_bytes=64, tag=f"codes{3 * t + a}")
-                for a in range(PASSES)
-            ]
-            for t in range(TILES)
-        ]
-        w1_plane = [
-            [keep.tile([P, 2 * P], U8, name=f"w1_plane{t}_{a}", align_bytes=64, tag=f"plane{3 * t + a}") for a in range(PASSES)]
-            for t in range(TILES)
-        ]
+        v_plane = buffer("v_plane", [P, S], U8)
+        v_codes = [buffer(f"v_codes{a}", [P, S], U32) for a in range(PASSES)]
+        w1_codes = [buffer(f"codes{n}", [P, 2 * P], U32) for n in range(STEPS)]
+        w1_plane = [buffer(f"plane{n}", [P, 2 * P], U8) for n in range(STEPS)]
 
         def gather_table(a):
-            for half in range(2):
-                nc.vector.tensor_copy(
-                    v_codes[a][:, half * BANK : (half + 1) * BANK],
-                    table[a][:].bitcast(U32).indirect(idx[:, half * 32 : (half + 1) * 32]),
-                )
+            for first in range(0, S, BANK):
+                entries = idx[:, first // PER_COL : (first + BANK) // PER_COL]
+                nc.vector.tensor_copy(v_codes[a][:, first : first + BANK], table[a][:].bitcast(U32).indirect(entries))
 
-        grouped_tag = {3: "table2", 4: "codes2", 5: "plane2"}
+        def rounded_tag(n):
+            last = PASSES - 1
+            if n < PASSES:
+                return f"rounded{n}"
+            if n < 2 * PASSES:
+                return [f"table{last}", f"codes{last}", f"plane{last}"][n - PASSES]
+            return f"raw{n - 2}"
 
         def quantize_w1(n):
-            t, a = divmod(n, PASSES)
-            tag = f"grouped{n}" if n < PASSES else grouped_tag.get(n, f"raw{n - 2}")
-            grouped = keep.tile([P, 2 * P, PACK], BF16, name=f"grouped{n}", align_bytes=64, tag=tag)
-            dst = grouped[:].rearrange("p (c i) j -> p c j i", i=4)
-            src = w1_raw[t][a][:].rearrange("p j u (c i) -> p (u c) j i", i=4)
+            rounded = buffer(rounded_tag(n), [P, 2 * P, PACK], BF16)
+            dst = rounded[:].rearrange("p (c run) i -> p c i run", run=RUN)
+            src = w1_raw[n][:].rearrange("p i u (c run) -> p (u c) i run", run=RUN)
             if n <= PASSES:
                 nc.vector.tensor_copy(out=dst, in_=src)
             else:
                 nc.scalar.copy(out=dst, in_=src)
             nc.vector.quantize_mx(
-                out=w1_codes[t][a][:].bitcast(FP8X4),
-                scales=w1_plane[t][a][:],
-                in_=grouped[:].rearrange("p c j -> p (c j)"),
+                out=w1_codes[n][:].bitcast(FP8X4),
+                scales=w1_plane[n][:],
+                in_=rounded[:].rearrange("p c i -> p (c i)"),
             )
 
         nc.vector.tensor_copy(v_plane[:], tab_plane[:].indirect(idx[:]))
         gather_table(0)
         for n in range(PASSES):
             quantize_w1(n)
-        gather_table(1)
-        gather_table(2)
+        for a in range(1, PASSES):
+            gather_table(a)
 
-        h = [keep.tile([P, S], F32, name=f"h{t}") for t in range(TILES)]
-        x_rows = keep.tile([P, PACK, PAIRS], BF16, name="x_rows", align_bytes=64)
-        turns_per_h = keep.tile([P, TILES], F32, name="turns_per_h")
-        nc.vector.tensor_scalar(turns_per_h[:], tune_sb[:], 1.0 / (2.0 * math.pi), None, ALU.mult)
-        whole_all = keep.tile([P, TILES * S], I32, name="whole_all", tag="table1", align_bytes=64)
-        turns = []
+        h = [sbuf.tile([P, S], F32, name=f"h{t}") for t in range(TILES)]
+        x_rows = buffer("x_rows", [P, PACK, PAIRS], BF16)
+        turns_per_h = sbuf.tile([P, TILES], F32, name="turns_per_h")
+        nc.gpsimd.tensor_scalar(turns_per_h[:], tune_sb[:], 1.0 / (2.0 * math.pi), 0.0, ALU.mult, ALU.add)
+        whole = buffer("table1", [P, TILES * S], I32)
 
         def contrast(t):
-            tags = [f"raw{3 * t + 4}" if t in (1, 2) else f"mag{t % 2}_0", f"mag{t % 2}_1"]
-            mag = [keep.tile([P, S], F32, name=f"mag{u}", align_bytes=64, tag=tags[u]) for u in range(2)]
-            for half in range(2):
-                cols = slice(half * BANK, (half + 1) * BANK)
+            ahead = PASSES * (t + 1) + LEAD - 1
+            tonal_tag = f"raw{ahead}" if 0 < t and ahead < STEPS else f"tonal{t % 2}"
+            mag = [buffer(tonal_tag, [P, S], F32), buffer(f"broad{t % 2}", [P, S], F32)]
+            for first in range(0, S, BANK):
+                cols = slice(first, first + BANK)
                 for u in range(2):
                     acc = psum.tile([P, BANK], F32, name="acc")
                     for a in range(PASSES):
+                        n = PASSES * t + a
                         nc.tensor.matmul_mx(
                             out=acc[:],
-                            lhsT=w1_codes[t][a][:, u * P : (u + 1) * P].bitcast(FP8X4),
-                            lhsT_scale=w1_plane[t][a][:, u * P : (u + 1) * P],
+                            lhsT=w1_codes[n][:, u * P : (u + 1) * P].bitcast(FP8X4),
+                            lhsT_scale=w1_plane[n][:, u * P : (u + 1) * P],
                             rhs=v_codes[a][:, cols].bitcast(FP8X4),
                             rhs_scale=v_plane[4 * a :, cols],
                             start=(a == 0),
@@ -159,59 +159,63 @@ def tile_list_blade_noise_scores_kernel(
                     nc.scalar.activation(out=mag[u][:, cols], in_=acc[:], func=ACT.Abs)
                 nc.vector.tensor_tensor(h[t][:, cols], mag[0][:, cols], mag[1][:, cols], ALU.subtract)
 
+        def second_pick_tag(t):
+            return rounded_tag(PASSES * (t + 2) - 1) if t + 1 < TILES else "pick2"
+
         def pairs(t):
-            pick1 = keep.tile([P, PAIRS], F32, name="pick1", tag="pick0", align_bytes=64)
-            pick2 = keep.tile([P, PAIRS], F32, name="pick2", tag=["plane2", "raw6", "raw9", "pick1"][t], align_bytes=64)
+            pick1 = buffer("pick1", [P, PAIRS], F32)
+            pick2 = buffer(second_pick_tag(t), [P, PAIRS], F32)
             nc.vector.tensor_copy(pick1[:], h[t][:].indirect(p1[:]))
             nc.vector.tensor_copy(pick2[:], h[t][:].indirect(p2[:]))
-            x_tile = keep.tile([P, PAIRS], BF16, name="x_tile", tag=f"x{t}", align_bytes=64)
+            x_tile = buffer(f"x{t}", [P, PAIRS], BF16)
             nc.vector.tensor_tensor(x_tile[:], pick1[:], pick2[:], ALU.max)
             for i in range(PACK):
                 nc.sync.dma_start(out=x_rows[32 * t : 32 * (t + 1), i, :], in_=x_tile[i:P:PACK, :])
 
         def whole_turns(t):
             nc.gpsimd.tensor_scalar(
-                whole_all[:, t * S : (t + 1) * S], h[t][:], turns_per_h[:, t : t + 1], 0.0, ALU.mult, ALU.add
+                whole[:, t * S : (t + 1) * S], h[t][:], turns_per_h[:, t : t + 1], 0.0, ALU.mult, ALU.add
             )
 
-        def reduce_turns(t, dst):
+        def left_turns(t, dst):
             nc.vector.scalar_tensor_tensor(
-                dst, h[t][:], turns_per_h[:, t : t + 1], whole_all[:, t * S : (t + 1) * S], ALU.mult, ALU.subtract
+                dst, h[t][:], turns_per_h[:, t : t + 1], whole[:, t * S : (t + 1) * S], ALU.mult, ALU.subtract
             )
-            turns.append(dst)
+            return dst
 
+        left = []
         done = PASSES
         for t in range(TILES):
             contrast(t)
             whole_turns(t)
-            upto = min(PASSES * (t + 2) + 2, PASSES * TILES)
+            upto = min(PASSES * (t + 2) + LEAD, STEPS)
             for n in range(done, upto):
                 quantize_w1(n)
             done = upto
             pairs(t)
             if t == 0:
-                turns_first = keep.tile([P, S], F32, name="turns_first", tag="plane2", align_bytes=64)
-                reduce_turns(0, turns_first[:])
-        turns_rest = keep.tile([P, (TILES - 1) * S], F32, name="turns_rest", tag="pick0", align_bytes=64)
+                left.append(left_turns(0, buffer(second_pick_tag(0), [P, S], F32)[:]))
+        left_rest = buffer("pick1", [P, (TILES - 1) * S], F32)
         for t in range(1, TILES):
-            reduce_turns(t, turns_rest[:, (t - 1) * S : t * S])
+            left.append(left_turns(t, left_rest[:, (t - 1) * S : t * S]))
 
-        wave = [keep.tile([P, S], F32, name=f"wave{t}", align_bytes=64, tag=["codes11", "wave1", "wave2", "wave3"][t]) for t in range(TILES)]
+        wave = [buffer(f"codes{STEPS - 1}" if t == 0 else f"wave{t}", [P, S], F32) for t in range(TILES)]
         for t in range(TILES):
-            nc.scalar.activation(out=wave[t][:], in_=turns[t], func=ACT.Sin, scale=2.0 * math.pi)
+            nc.scalar.activation(out=wave[t][:], in_=left[t], func=ACT.Sin, scale=2.0 * math.pi)
 
-        x_grouped = keep.tile([P, PAIRS, PACK], BF16, name="x_grouped", align_bytes=64)
+        x_rounded = buffer("x_rounded", [P, PAIRS, PACK], BF16)
         nc.vector.tensor_copy(
-            out=x_grouped[:].rearrange("p (c i) j -> p c j i", i=4),
-            in_=x_rows[:].rearrange("p j (c i) -> p c j i", i=4),
+            out=x_rounded[:].rearrange("p (c run) i -> p c i run", run=RUN),
+            in_=x_rows[:].rearrange("p i (c run) -> p c i run", run=RUN),
         )
-        x_codes = keep.tile([P, PAIRS], U32, name="x_codes", align_bytes=64)
-        x_plane = keep.tile([P, PAIRS], U8, name="x_plane", align_bytes=64)
-
+        x_codes = buffer("x_codes", [P, PAIRS], U32)
+        x_plane = buffer("x_plane", [P, PAIRS], U8)
         nc.vector.quantize_mx(
-            out=x_codes[:].bitcast(FP8X4), scales=x_plane[:], in_=x_grouped[:].rearrange("p c j -> p (c j)")
+            out=x_codes[:].bitcast(FP8X4), scales=x_plane[:], in_=x_rounded[:].rearrange("p c i -> p (c i)")
         )
-        y = [keep.tile([P, PAIRS], F32, name=f"y{t}") for t in range(TILES)]
+
+        y_by_vector = 2
+        y = []
 
         def second_stage(t):
             acc = psum.tile([P, BANK], F32, name="acc")
@@ -224,22 +228,32 @@ def tile_list_blade_noise_scores_kernel(
                 start=True,
                 stop=True,
             )
-            nc.scalar.copy(out=y[t][:], in_=acc[:])
+            y_tile = sbuf.tile([P, PAIRS], F32, name="y_tile", tag=f"y{t}")
+            if t < y_by_vector:
+                nc.vector.tensor_copy(out=y_tile[:], in_=acc[:])
+            else:
+                nc.scalar.copy(out=y_tile[:], in_=acc[:])
+            y.append(y_tile)
 
-        up_all = keep.tile([P, TILES * S], F32, name="up_all", tag="table0", align_bytes=64)
-        second_stage(0)
+        up_all = buffer("table0", [P, TILES * S], F32)
+        for t in range(y_by_vector):
+            second_stage(t)
         for t in range(TILES):
-            if t + 1 < TILES:
-                second_stage(t + 1)
-            for half in range(2):
-                cols = slice(half * BANK, (half + 1) * BANK)
-                up = up_all[:, t * S + half * BANK : t * S + (half + 1) * BANK]
-                for quarter in range(2):
-                    first = 32 * half + 16 * quarter
-                    nc.vector.tensor_copy(
-                        up[:, quarter * 256 : (quarter + 1) * 256], y[t][:].indirect(p3[:, first : first + 16])
-                    )
-                nc.scalar.activation(out=up, in_=up, func=ACT.Tanh)
-                engine = nc.gpsimd if t + 1 < TILES else nc.vector
-                engine.tensor_tensor(wave[t][:, cols], wave[t][:, cols], up, ALU.mult)
+            last = t + 1 == TILES
+            width = UP_SLICE if last else BANK
+            multiplier = nc.vector if last else nc.gpsimd
+            later = t + y_by_vector
+            for first in range(0, S, width):
+                cols = slice(first, first + width)
+                up = up_all[:, t * S + first : t * S + first + width]
+                frees_later = first == 0 and later < TILES
+                picked = sbuf.tile([P, BANK], F32, name="picked", tag=f"y{later}")[:] if frees_later else up
+                for at in range(0, width, UP_SLICE):
+                    col = (first + at) // PER_COL
+                    entries = p3[:, col : col + UP_SLICE // PER_COL]
+                    nc.vector.tensor_copy(picked[:, at : at + UP_SLICE], y[t][:].indirect(entries))
+                nc.scalar.activation(out=up, in_=picked, func=ACT.Tanh)
+                if frees_later:
+                    second_stage(later)
+                multiplier.tensor_tensor(wave[t][:, cols], wave[t][:, cols], up, ALU.mult)
                 nc.sync.dma_start(out=out[t * P : (t + 1) * P, cols], in_=wave[t][:, cols])

import math
from contextlib import ExitStack

import concourse.mybir as mybir

K, H, T, S, PAIRS = 1536, 512, 4096, 1024, 512
P = 128
PACK = 4
K_PASS = P * PACK
PASSES = K // K_PASS
TILES = H // P
STEPS = TILES * PASSES
LEAD = 2
BANK = 512
QUADS = 4
PER_COL = 16
UP_SLICE = PAIRS // 2
RUN = 4

FLOPS = 2 * K * (2 * H) * S + 2 * H * H * PAIRS

F32 = mybir.dt.float32
BF16 = mybir.dt.bfloat16
I32 = mybir.dt.int32
U32 = mybir.dt.uint32
U16 = mybir.dt.uint16
U8 = mybir.dt.uint8
FP8X4 = mybir.dt.float8_e4m3fn_x4
FP4X4 = mybir.dt.float4_e2m1fn_x4
ALU = mybir.AluOpType
ACT = mybir.ActivationFunctionType


def tile_list_blade_noise_scores_kernel(
    tc, tab_words, tab_scales, offs, w1, pos1, pos2, w2_words, w2_scales, pos3, tune, out
):
    nc = tc.nc
    with ExitStack() as ctx:
        sbuf = ctx.enter_context(tc.tile_pool(name="sbuf", bufs=1))
        psum = ctx.enter_context(tc.psum_pool(name="psum", bufs=8))

        def buffer(tag, shape, dtype):
            return sbuf.tile(shape, dtype, name=tag, tag=tag, align_bytes=64)

        idx = sbuf.tile([P, S // PER_COL], U16, name="idx")
        p1 = sbuf.tile([P, PAIRS // PER_COL], U16, name="p1")
        p2 = sbuf.tile([P, PAIRS // PER_COL], U16, name="p2")
        p3 = sbuf.tile([P, S // PER_COL], U16, name="p3")

        tab_plane = buffer("tab_plane", [P, T], U8)
        w2_plane = buffer("w2_plane", [P, H], U8)
        nc.vector.memset(tab_plane[:].bitcast(I32), 0)
        nc.vector.memset(w2_plane[:].bitcast(I32), 0)
        for quad in range(QUADS):
            nc.sync.dma_start(
                out=tab_plane[32 * quad : 32 * quad + 4 * PASSES, :].bitcast(I32),
                in_=tab_scales[:, 4 * quad : 4 * quad + 4, :].bitcast(I32),
            )

        table = [buffer(f"table{a}", [P, T], I32) for a in range(PASSES)]
        w1_raw = [buffer(f"raw{n}", [P, PACK, 2, P], F32) for n in range(STEPS)]

        def load_table(a):
            nc.sync.dma_start(out=table[a][:], in_=tab_words[a].rearrange("p t i -> p (t i)").bitcast(I32))

        def load_w1(t):
            for a in range(PASSES):
                rows = w1[a * K_PASS : (a + 1) * K_PASS, :].rearrange("(p i) (u c) -> p (i u) c", i=PACK, u=2)
                nc.sync.dma_start(
                    out=w1_raw[PASSES * t + a][:].rearrange("p i u c -> p (i u) c"),
                    in_=rows[:, :, t * P : (t + 1) * P],
                )

        load_table(0)
        nc.sync.dma_start(idx[:], offs)
        load_w1(0)
        for a in range(1, PASSES):
            load_table(a)
        nc.sync.dma_start(p1[:], pos1)
        nc.sync.dma_start(p2[:], pos2)
        tune_sb = sbuf.tile([P, TILES], F32, name="tune_sb")
        with nc.allow_non_contiguous_dma(reason="512 values: tune[128 t + p] goes to [p, t]"):
            nc.sync.dma_start(out=tune_sb[:], in_=tune.rearrange("(t p) -> p t", p=P))
        for t in range(1, TILES):
            load_w1(t)
        nc.sync.dma_start(p3[:], pos3)
        w2_codes = buffer("w2_codes", [P, 2 * H], U8)
        nc.sync.dma_start(out=w2_codes[:].bitcast(I32), in_=w2_words[0].bitcast(I32))
        for quad in range(QUADS):
            nc.sync.dma_start(
                out=w2_plane[32 * quad : 32 * quad + 4, :].bitcast(I32),
                in_=w2_scales[0, 4 * quad : 4 * quad + 4, :].bitcast(I32),
            )

        v_plane = buffer("v_plane", [P, S], U8)
        v_codes = [buffer(f"v_codes{a}", [P, S], U32) for a in range(PASSES)]
        w1_codes = [buffer(f"codes{n}", [P, 2 * P], U32) for n in range(STEPS)]
        w1_plane = [buffer(f"plane{n}", [P, 2 * P], U8) for n in range(STEPS)]

        def gather_table(a):
            for first in range(0, S, BANK):
                entries = idx[:, first // PER_COL : (first + BANK) // PER_COL]
                nc.vector.tensor_copy(v_codes[a][:, first : first + BANK], table[a][:].bitcast(U32).indirect(entries))

        def rounded_tag(n):
            last = PASSES - 1
            if n < PASSES:
                return f"rounded{n}"
            if n < 2 * PASSES:
                return [f"table{last}", f"codes{last}", f"plane{last}"][n - PASSES]
            return f"raw{n - 2}"

        def quantize_w1(n):
            rounded = buffer(rounded_tag(n), [P, 2 * P, PACK], BF16)
            dst = rounded[:].rearrange("p (c run) i -> p c i run", run=RUN)
            src = w1_raw[n][:].rearrange("p i u (c run) -> p (u c) i run", run=RUN)
            if n <= PASSES:
                nc.vector.tensor_copy(out=dst, in_=src)
            else:
                nc.scalar.copy(out=dst, in_=src)
            nc.vector.quantize_mx(
                out=w1_codes[n][:].bitcast(FP8X4),
                scales=w1_plane[n][:],
                in_=rounded[:].rearrange("p c i -> p (c i)"),
            )

        nc.vector.tensor_copy(v_plane[:], tab_plane[:].indirect(idx[:]))
        gather_table(0)
        for n in range(PASSES):
            quantize_w1(n)
        for a in range(1, PASSES):
            gather_table(a)

        h = [sbuf.tile([P, S], F32, name=f"h{t}") for t in range(TILES)]
        x_rows = buffer("x_rows", [P, PACK, PAIRS], BF16)
        turns_per_h = sbuf.tile([P, TILES], F32, name="turns_per_h")
        nc.gpsimd.tensor_scalar(turns_per_h[:], tune_sb[:], 1.0 / (2.0 * math.pi), 0.0, ALU.mult, ALU.add)
        whole = buffer("table1", [P, TILES * S], I32)

        def contrast(t):
            ahead = PASSES * (t + 1) + LEAD - 1
            tonal_tag = f"raw{ahead}" if 0 < t and ahead < STEPS else f"tonal{t % 2}"
            mag = [buffer(tonal_tag, [P, S], F32), buffer(f"broad{t % 2}", [P, S], F32)]
            for first in range(0, S, BANK):
                cols = slice(first, first + BANK)
                for u in range(2):
                    acc = psum.tile([P, BANK], F32, name="acc")
                    for a in range(PASSES):
                        n = PASSES * t + a
                        nc.tensor.matmul_mx(
                            out=acc[:],
                            lhsT=w1_codes[n][:, u * P : (u + 1) * P].bitcast(FP8X4),
                            lhsT_scale=w1_plane[n][:, u * P : (u + 1) * P],
                            rhs=v_codes[a][:, cols].bitcast(FP8X4),
                            rhs_scale=v_plane[4 * a :, cols],
                            start=(a == 0),
                            stop=(a == PASSES - 1),
                        )
                    nc.scalar.activation(out=mag[u][:, cols], in_=acc[:], func=ACT.Abs)
                nc.vector.tensor_tensor(h[t][:, cols], mag[0][:, cols], mag[1][:, cols], ALU.subtract)

        def second_pick_tag(t):
            return rounded_tag(PASSES * (t + 2) - 1) if t + 1 < TILES else "pick2"

        def pairs(t):
            pick1 = buffer("pick1", [P, PAIRS], F32)
            pick2 = buffer(second_pick_tag(t), [P, PAIRS], F32)
            nc.vector.tensor_copy(pick1[:], h[t][:].indirect(p1[:]))
            nc.vector.tensor_copy(pick2[:], h[t][:].indirect(p2[:]))
            x_tile = buffer(f"x{t}", [P, PAIRS], BF16)
            nc.vector.tensor_tensor(x_tile[:], pick1[:], pick2[:], ALU.max)
            for i in range(PACK):
                nc.sync.dma_start(out=x_rows[32 * t : 32 * (t + 1), i, :], in_=x_tile[i:P:PACK, :])

        def whole_turns(t):
            nc.gpsimd.tensor_scalar(
                whole[:, t * S : (t + 1) * S], h[t][:], turns_per_h[:, t : t + 1], 0.0, ALU.mult, ALU.add
            )

        def left_turns(t, dst):
            nc.vector.scalar_tensor_tensor(
                dst, h[t][:], turns_per_h[:, t : t + 1], whole[:, t * S : (t + 1) * S], ALU.mult, ALU.subtract
            )
            return dst

        left = []
        done = PASSES
        for t in range(TILES):
            contrast(t)
            whole_turns(t)
            upto = min(PASSES * (t + 2) + LEAD, STEPS)
            for n in range(done, upto):
                quantize_w1(n)
            done = upto
            pairs(t)
            if t == 0:
                left.append(left_turns(0, buffer(second_pick_tag(0), [P, S], F32)[:]))
        left_rest = buffer("pick1", [P, (TILES - 1) * S], F32)
        for t in range(1, TILES):
            left.append(left_turns(t, left_rest[:, (t - 1) * S : t * S]))

        wave = [buffer(f"codes{STEPS - 1}" if t == 0 else f"wave{t}", [P, S], F32) for t in range(TILES)]
        for t in range(TILES):
            nc.scalar.activation(out=wave[t][:], in_=left[t], func=ACT.Sin, scale=2.0 * math.pi)

        x_rounded = buffer("x_rounded", [P, PAIRS, PACK], BF16)
        nc.vector.tensor_copy(
            out=x_rounded[:].rearrange("p (c run) i -> p c i run", run=RUN),
            in_=x_rows[:].rearrange("p i (c run) -> p c i run", run=RUN),
        )
        x_codes = buffer("x_codes", [P, PAIRS], U32)
        x_plane = buffer("x_plane", [P, PAIRS], U8)
        nc.vector.quantize_mx(
            out=x_codes[:].bitcast(FP8X4), scales=x_plane[:], in_=x_rounded[:].rearrange("p c i -> p (c i)")
        )

        y_by_vector = 2
        y = []

        def second_stage(t):
            acc = psum.tile([P, BANK], F32, name="acc")
            nc.tensor.matmul_mx(
                out=acc[:],
                lhsT=w2_codes[:, 2 * t * P : 2 * (t + 1) * P].bitcast(FP4X4),
                lhsT_scale=w2_plane[:, t * P : (t + 1) * P],
                rhs=x_codes[:].bitcast(FP8X4),
                rhs_scale=x_plane[:],
                start=True,
                stop=True,
            )
            y_tile = sbuf.tile([P, PAIRS], F32, name="y_tile", tag=f"y{t}")
            if t < y_by_vector:
                nc.vector.tensor_copy(out=y_tile[:], in_=acc[:])
            else:
                nc.scalar.copy(out=y_tile[:], in_=acc[:])
            y.append(y_tile)

        up_all = buffer("table0", [P, TILES * S], F32)
        for t in range(y_by_vector):
            second_stage(t)
        for t in range(TILES):
            last = t + 1 == TILES
            width = UP_SLICE if last else BANK
            multiplier = nc.vector if last else nc.gpsimd
            later = t + y_by_vector
            for first in range(0, S, width):
                cols = slice(first, first + width)
                up = up_all[:, t * S + first : t * S + first + width]
                frees_later = first == 0 and later < TILES
                picked = sbuf.tile([P, BANK], F32, name="picked", tag=f"y{later}")[:] if frees_later else up
                for at in range(0, width, UP_SLICE):
                    col = (first + at) // PER_COL
                    entries = p3[:, col : col + UP_SLICE // PER_COL]
                    nc.vector.tensor_copy(picked[:, at : at + UP_SLICE], y[t][:].indirect(entries))
                nc.scalar.activation(out=up, in_=picked, func=ACT.Tanh)
                if frees_later:
                    second_stage(later)
                multiplier.tensor_tensor(wave[t][:, cols], wave[t][:, cols], up, ALU.mult)
                nc.sync.dma_start(out=out[t * P : (t + 1) * P, cols], in_=wave[t][:, cols])
